import numpy as np
CORES = [50,55,434,439,178,183,306,311]
N = 8
def setup_inputs(rng):
    return {"x": rng.standard_normal((N, 128, 32), dtype=np.float32)}
def reference(x):
    g = np.concatenate(list(x), axis=1)
    return {"y": np.broadcast_to(g, (N,) + g.shape)}

from concourse.bass import DstId, RemoteDMATransfer

N_RANKS = 8

SCRATCH = {
    "land": ("dram", [N_RANKS, 128, 32], "float32"),
}
SEMAPHORES = ["ld", "go1", "go2", "sent", "gst", "st"] + ["arr%d" % j for j in range(N_RANKS)]


def _bits(m):
    return [1 << i for i in range(m.bit_length()) if (m >> i) & 1]


def _plan(c, T, topo):
    others = [d for d in T.cores if d != c]
    mate = [d for d in others if topo.host(d) == topo.host(c) and topo.chip(d) == topo.chip(c)]
    plane = [d for d in others if topo.same_plane(c, d)]
    far = [d for d in others if topo.rack(topo.host(d)) != topo.rack(topo.host(c)) and topo.may_write(c, d)]
    cable = [d for d in far if topo.die(d) == topo.die(c)][:1]
    off_mask = topo.mask(c, cable[0])
    for d in plane:
        off_mask &= topo.mask(c, d)
    off = _bits(off_mask)
    stay = [b for b in _bits(topo.mask(c, mate[0])) if b not in off]
    h = len(off) // 2
    own = T.rank_of(c)
    came = T.rank_of(cable[0])
    send = [(own, cable, off[:h]), (own, plane, off[h:]), (own, mate, stay)]
    fwd = [(came, plane, off), (came, mate, stay)]
    return send, fwd


def rank_program(g, core, T, topo):
    rank = T.rank_of(core)
    if rank is None:
        return
    w = T.x.shape[1]
    send, fwd = _plan(core, T, topo)

    lands = {}
    for c in T.cores:
        s, f = _plan(c, T, topo)
        for second, trs in ((False, s), (True, f)):
            for blk, dsts, eng in trs:
                if core in dsts:
                    lands[blk] = (len(eng), second, c)

    def arr(j):
        return T.sem["arr%d" % j]

    def call(trs):
        out = []
        for blk, dsts, eng in trs:
            ids = []
            for d in dsts:
                rid, pid = topo.addr(d, core)
                ids.append(DstId(rid=rid, pnc=pid))
            out.append(RemoteDMATransfer(dst_ids=ids, dma_engine_mask=sum(eng), remote_sem=arr(blk),
                                         srcs=[T.land[blk]], dsts=[T.land[blk] for _ in dsts]))
        g.remote_dma_fused(out, local_sem=T.sem.sent)
        return sum(len(eng) for _, _, eng in trs)

    def cols(j):
        return T.y[:, w * j:w * (j + 1)]

    on_chip = lambda c: topo.host(c) == topo.host(core) and topo.chip(c) == topo.chip(core)
    came = fwd[0][0]
    first = [j for j in lands if not lands[j][1]]
    second = [j for j in lands if lands[j][1]]
    mate_blk = [j for j in first if on_chip(lands[j][2])][0]
    plane_blk = [j for j in first if j != mate_blk and j != came]
    mate_fwd = [j for j in second if on_chip(lands[j][2])][0]
    diag_blk = [j for j in second if j != mate_fwd]

    n_st = [0]

    def store(q, j):
        q.wait_ge(arr(j), lands[j][0])
        q.dma_start(cols(j), T.land[j]).then_inc(T.sem.st, 16)
        n_st[0] += 16

    g.sync.dma_start(T.land[rank], T.x[:, :]).then_inc(T.sem.ld, 16)
    g.sync.wait_ge(T.sem.go2, 1)
    store(g.sync, plane_blk[0])
    store(g.sync, mate_fwd)
    store(g.sync, diag_blk[0])

    g.scalar.wait_ge(T.sem.go1, 1)
    g.scalar.dma_start(cols(rank), T.x[:, :]).then_inc(T.sem.st, 16)
    n_st[0] += 16
    store(g.scalar, mate_blk)
    g.scalar.wait_ge(T.sem.go2, 1)
    store(g.scalar, plane_blk[1])
    store(g.scalar, diag_blk[1])

    g.wait_ge(T.sem.ld, 16)
    left = call(send)
    g.sem_inc(T.sem.go1, 1)
    g.wait_ge(arr(came), lands[came][0])
    left += call(fwd)
    g.sem_inc(T.sem.go2, 1)
    g.dma_start(cols(came), T.land[came]).then_inc(T.sem.gst, 16)
    g.wait_ge(T.sem.sent, left)
    g.wait_ge(T.sem.gst, 16)
    g.wait_ge(T.sem.st, n_st[0])
